import numpy as np
import ml_dtypes


def mxq(x, axis, fmt="e4m3"):
    dtype, down = {"e4m3": (ml_dtypes.float8_e4m3fn, 7), "e5m2": (ml_dtypes.float8_e5m2, 14)}[fmt]
    v = np.moveaxis(np.asarray(x, np.float32).astype(ml_dtypes.bfloat16).astype(np.float64), axis, -1)
    blocks = v.reshape(v.shape[:-1] + (-1, 32))
    amax = np.abs(blocks).max(-1, keepdims=True)
    byte = np.maximum(np.where(amax > 0, np.frexp(amax)[1] - 1 + 127, 0) - down, 1)
    scale = np.exp2(byte - 127.0)
    codes = (blocks / scale).astype(np.float32).astype(dtype).astype(np.float64)
    return np.moveaxis((codes * scale).reshape(v.shape), -1, axis)


WIDE = False


def mx_kscale(k):
    if not WIDE:
        return np.ones(k)
    levels = np.array([10, -10, 5, -5, 0])
    if k % 512:
        return np.exp2(np.random.permutation(np.resize(levels, k // 32))).repeat(32)
    a = np.empty((k // 512, 16))
    for p in range(k // 512):
        a[p, :8] = np.random.permutation(np.resize(levels, 8))
        for g in range(8):
            far = levels[np.abs(levels - a[p, g]) >= 10]
            a[p, g + 8] = far[np.random.randint(len(far))]
    return np.exp2(a.ravel()).repeat(32)


def f64(x):
    return np.asarray(x).astype(np.float64)


def striped(idx):
    return np.tile(np.asarray(idx).reshape(-1, 16).T, (8, 1)).astype(np.uint16)


def unstriped(offs):
    return offs[:16].T.reshape(-1).astype(np.int64)


E2M1 = np.array([0.0, 0.5, 1.0, 1.5, 2.0, 3.0, 4.0, 6.0, -0.0, -0.5, -1.0, -1.5, -2.0, -3.0, -4.0, -6.0])


def pack_weight(w, fmt):
    k, n = w.shape
    w = f64(np.asarray(w, np.float32).astype(ml_dtypes.bfloat16)).reshape(k // 32, 32, n)
    amax = np.abs(w).max(1)
    if fmt == "e4m3":
        byte = np.frexp(amax)[1] - 1 + 127 - 7
    else:
        mant, ex = np.frexp(amax / 6.0)
        byte = np.where(mant > 0.5, ex, ex - 1) + 127
    byte = np.clip(np.where(amax > 0, byte, 1), 1, 254)
    scaled = (w * np.exp2(127.0 - byte)[:, None, :]).reshape(k, n).astype(np.float32)
    by_word = np.ascontiguousarray(scaled.reshape(k // 512, 128, 4, n).transpose(0, 1, 3, 2))
    if fmt == "e4m3":
        words = by_word.astype(ml_dtypes.float8_e4m3fn).view(np.uint8)
    else:
        c = by_word.astype(ml_dtypes.float4_e2m1fn).view(np.uint8) & 0xF
        words = (c[..., 0::2] | (c[..., 1::2] << 4)).reshape(k // 512, 128, 2 * n)
    return np.ascontiguousarray(words), np.ascontiguousarray(byte.astype(np.uint8).reshape(k // 512, 16, n))


def unpack_weight(words, scales, fmt):
    g, _, n = scales.shape
    words = np.ascontiguousarray(words).reshape(g, 128, n, -1)
    if fmt == "e4m3":
        vals = words.view(ml_dtypes.float8_e4m3fn).astype(np.float64)
    else:
        nib = np.empty((g, 128, n, 4), np.uint8)
        nib[..., 0::2] = words & 0xF
        nib[..., 1::2] = words >> 4
        vals = E2M1[nib]
    vals = vals * np.repeat(np.exp2(scales.astype(np.float64) - 127.0), 8, axis=1)[..., None]
    return vals.transpose(0, 1, 3, 2).reshape(g * 512, n)


D, T, I, J, U, M, N = 512, 2048, 512, 512, 1024, 512, 64


def setup_inputs():
    n = np.random.standard_normal
    idx = np.random.permutation(T)[:I]
    idx2 = np.random.permutation(U)[:J]
    idx3 = np.random.permutation(U)[:J]
    idx4 = np.random.permutation(M)[:N]
    fd = mx_kscale(D)
    keysp = pack_weight(n((D, T)) / fd[:, None], "e4m3")
    return {
        "keys_words": keysp[0],
        "keys_scales": keysp[1],
        "notes": (n((D, U)) * 1.0 / np.sqrt(D) * fd[:, None]).astype(np.float32),
        "old": (1.0 * n((I, M))).astype(np.float32),
        "offs": striped(idx),
        "offs2": striped(idx2),
        "offs3": striped(idx3),
        "offs4": striped(idx4),
    }


def reference(keys_words, keys_scales, notes, old, offs, offs2, offs3, offs4):
    idx = unstriped(offs)
    idx2 = unstriped(offs2)
    idx3 = unstriped(offs3)
    idx4 = unstriped(offs4)
    keysu = unpack_weight(keys_words, keys_scales, "e4m3")
    keysidxg = keysu[:, idx]
    notesq = mxq(f64(notes), 0, "e4m3")
    g1 = keysidxg.T @ notesq
    g0 = g1[:, idx2] - g1[:, idx3]
    rb0 = g0.reshape(I, N, J // N).max(axis=2)
    gf = np.zeros((I, M))
    gf[:, idx4] = rb0
    y = f64(old) + gf
    return y

@@ -1,0 +1,179 @@
+from contextlib import ExitStack
+
+import concourse.mybir as mybir
+
+D, T, I, J, U, M, N = 512, 2048, 512, 512, 1024, 512, 64
+FLOPS = 2 * D * I * U
+
+F32 = mybir.dt.float32
+BF16 = mybir.dt.bfloat16
+I32 = mybir.dt.int32
+U32 = mybir.dt.uint32
+U16 = mybir.dt.uint16
+U8 = mybir.dt.uint8
+FP8X4 = mybir.dt.float8_e4m3fn_x4
+ALU = mybir.AluOpType
+COPY = mybir.ActivationFunctionType.Copy
+
+P = 128
+PACK = 4
+BANK = 512
+RUN = J // N
+ROW_TILES = I // P
+CHUNKS = (256, 256, 256, 128, 128)
+
+
+def tile_attend_tab_looked_runsput_kernel(tc, keys_words, keys_scales, notes, old, offs, offs2, offs3, offs4, out):
+    nc = tc.nc
+    with ExitStack() as ctx:
+        lists = ctx.enter_context(tc.tile_pool(name="lists", bufs=1))
+        keep = ctx.enter_context(tc.tile_pool(name="keep", bufs=1))
+        psum = ctx.enter_context(tc.psum_pool(name="psum", bufs=1))
+
+        idx = lists.tile([P, I // 16], U16, name="idx")
+        idx2 = lists.tile([P, J // 16], U16, name="idx2")
+        idx3 = lists.tile([P, J // 16], U16, name="idx3")
+        idx4 = lists.tile([P, N // 16], U16, name="idx4")
+
+        pool_words = keep.tile([P, T], U32, name="pool_words", align_bytes=64)
+        pool_scales = keep.tile([P, T], U8, name="pool_scales", align_bytes=64)
+        key_words = keep.tile([P, I], U32, name="key_words", align_bytes=64)
+        key_scales = keep.tile([P, I], U8, name="key_scales", align_bytes=64)
+
+        starts = [sum(CHUNKS[:c]) for c in range(len(CHUNKS))]
+        raw = [keep.tile([P, PACK, w], F32, name=f"raw{c}") for c, w in enumerate(CHUNKS)]
+        notes_v = notes.rearrange("(p j) u -> p j u", j=PACK)
+
+        def load_notes(c):
+            nc.sync.dma_start(out=raw[c][:], in_=notes_v[:, :, starts[c] : starts[c] + CHUNKS[c]])
+
+        nc.gpsimd.memset(pool_scales[:].bitcast(I32), 0)
+        load_notes(0)
+        for q in range(4):
+            nc.sync.dma_start(
+                out=pool_scales[32 * q : 32 * q + 4, :].bitcast(I32),
+                in_=keys_scales[0, 4 * q : 4 * q + 4, :].bitcast(I32),
+            )
+        nc.sync.dma_start(idx[:], offs)
+        nc.sync.dma_start(
+            out=pool_words[:].bitcast(I32),
+            in_=keys_words[0].rearrange("p n t -> p (n t)").bitcast(I32),
+        )
+        for c in range(1, len(CHUNKS)):
+            load_notes(c)
+        nc.sync.dma_start(idx3[:], offs3)
+        nc.sync.dma_start(idx2[:], offs2)
+        nc.sync.dma_start(idx4[:], offs4)
+        prev = [keep.tile([P, M], F32, name=f"prev{t}") for t in range(ROW_TILES)]
+        for t in range(ROW_TILES):
+            nc.sync.dma_start(out=prev[t][:], in_=old[t * P : (t + 1) * P, :])
+
+        placed = [keep.tile([P, M], F32, name=f"placed{t}") for t in range(ROW_TILES)]
+        for t in range(ROW_TILES):
+            nc.gpsimd.memset(placed[t][:], 0.0)
+
+        wide = [keep.tile([P, U], F32, name=f"wide{t}") for t in range(ROW_TILES)]
+        note_words = [keep.tile([P, w], U32, name=f"note_words{c}", align_bytes=64) for c, w in enumerate(CHUNKS)]
+        note_scales = [keep.tile([P, w], U8, name=f"note_scales{c}", align_bytes=64) for c, w in enumerate(CHUNKS)]
+        sums = {}
+
+        def quantise(c):
+            w = CHUNKS[c]
+            grouped = keep.tile([P, w, PACK], BF16, name=f"grouped{c}", align_bytes=64)
+            nc.vector.tensor_copy(
+                out=grouped[:].rearrange("p (c i) t -> p c t i", i=4),
+                in_=raw[c][:].rearrange("p t (c i) -> p c t i", i=4),
+            )
+            nc.vector.quantize_mx(
+                out=note_words[c][:].bitcast(FP8X4),
+                scales=note_scales[c][:],
+                in_=grouped[:].rearrange("p w t -> p (w t)"),
+            )
+
+        SPAN = 256
+        banks = {
+            (g, h): psum.tile([P, BANK], F32, name=f"bank{g}_{h}") for g in range(U // SPAN) for h in range(ROW_TILES // 2)
+        }
+
+        def multiply(c):
+            w = CHUNKS[c]
+            g, inner = divmod(starts[c], SPAN)
+            for t in range(ROW_TILES):
+                first = (t % 2) * SPAN + inner
+                rows = slice(t * P, (t + 1) * P)
+                nc.tensor.matmul_mx(
+                    out=banks[g, t // 2][:, first : first + w],
+                    lhsT=key_words[:, rows].bitcast(FP8X4),
+                    lhsT_scale=key_scales[:, rows],
+                    rhs=note_words[c][:].bitcast(FP8X4),
+                    rhs_scale=note_scales[c][:],
+                    start=True,
+                    stop=True,
+                )
+
+        def evacuate(g, t):
+            source = banks[g, t // 2][:, (t % 2) * SPAN : (t % 2 + 1) * SPAN]
+            target = wide[t][:, g * SPAN : (g + 1) * SPAN]
+            if g == U // SPAN - 1 and t > 0:
+                nc.vector.tensor_copy(out=target, in_=source)
+            else:
+                nc.scalar.copy(out=target, in_=source)
+
+        quantise(0)
+        nc.vector.tensor_copy(key_scales[:], pool_scales[:].indirect(idx[:]))
+        for t in range(ROW_TILES):
+            nc.vector.tensor_copy(key_words[:, t * P : (t + 1) * P], pool_words[:].indirect(idx[:, t * 8 : (t + 1) * 8]))
+        for c in range(len(CHUNKS)):
+            if c > 0:
+                quantise(c)
+            multiply(c)
+
+        second = [keep.tile([P, J], F32, name=f"second{t}") for t in range(ROW_TILES)]
+        diff = [keep.tile([P, J], F32, name=f"diff{t}") for t in range(ROW_TILES)]
+        best = [keep.tile([P, N], F32, name=f"best{t}") for t in range(ROW_TILES)]
+        result = [keep.tile([P, M], F32, name=f"result{t}") for t in range(ROW_TILES)]
+
+        minuend = keep.tile([P, J], F32, name="minuend")
+        last = ROW_TILES - 1
+
+        def look_up(t, lo, hi):
+            cols = slice(lo, hi)
+            entries = slice(lo // 16, hi // 16)
+            nc.scalar.activation(second[t][:, cols], wide[t][:].indirect(idx3[:, entries]), COPY)
+            if t == last:
+                nc.scalar.activation(minuend[:, cols], wide[t][:].indirect(idx2[:, entries]), COPY)
+                nc.vector.tensor_tensor(diff[t][:, cols], minuend[:, cols], second[t][:, cols], ALU.subtract)
+            else:
+                nc.vector.tensor_tensor(diff[t][:, cols], wide[t][:].indirect(idx2[:, entries]), second[t][:, cols], ALU.subtract)
+
+        def largest(t, lo, hi):
+            nc.vector.tensor_reduce(
+                best[t][:, lo // RUN : hi // RUN],
+                diff[t][:, lo:hi].rearrange("p (n r) -> p n r", r=RUN),
+                axis=mybir.AxisListType.X,
+                op=ALU.max,
+            )
+
+        def place(t):
+            nc.scalar.activation(placed[t][:].indirect(idx4[:]), best[t][:], COPY)
+
+        def finish(t, lo, hi, queue):
+            nc.vector.tensor_tensor(result[t][:, lo:hi], prev[t][:, lo:hi], placed[t][:, lo:hi], ALU.add)
+            queue.dma_start(out=out[t * P : (t + 1) * P, lo:hi], in_=result[t][:, lo:hi])
+
+        for t in range(ROW_TILES):
+            evacuate(U // SPAN - 1, t)
+        for t in range(ROW_TILES):
+            for g in range(U // SPAN - 1):
+                evacuate(g, t)
+            halves = [(0, J // 2), (J // 2, J)] if t in (0, last) else [(0, J)]
+            for lo, hi in halves:
+                look_up(t, lo, hi)
+            if 0 < t < last:
+                finish(t - 1, 0, M, nc.sync)
+            for lo, hi in halves:
+                largest(t, lo, hi)
+            place(t)
+        finish(last - 1, 0, M, nc.sync)
+        finish(last, 0, M // 2, nc.sync)
+        finish(last, M // 2, M, nc.scalar)

@@ -20,7 +20,8 @@ PACK = 4
 BANK = 512
 RUN = J // N
 ROW_TILES = I // P
-CHUNKS = (256, 256, 256, 128, 128)
+LAST = ROW_TILES - 1
+CHUNKS = (512, 256, 256)
 
 
 def tile_attend_tab_looked_runsput_kernel(tc, keys_words, keys_scales, notes, old, offs, offs2, offs3, offs4, out):
@@ -41,11 +42,11 @@ def tile_attend_tab_looked_runsput_kernel(tc, keys_words, keys_scales, notes, ol
         key_scales = keep.tile([P, I], U8, name="key_scales", align_bytes=64)
 
         starts = [sum(CHUNKS[:c]) for c in range(len(CHUNKS))]
-        raw = [keep.tile([P, PACK, w], F32, name=f"raw{c}") for c, w in enumerate(CHUNKS)]
-        notes_v = notes.rearrange("(p j) u -> p j u", j=PACK)
+        raw = [keep.tile([P, PACK, width], F32, name=f"raw{c}") for c, width in enumerate(CHUNKS)]
+        notes_by_word = notes.rearrange("(p j) u -> p j u", j=PACK)
 
         def load_notes(c):
-            nc.sync.dma_start(out=raw[c][:], in_=notes_v[:, :, starts[c] : starts[c] + CHUNKS[c]])
+            nc.sync.dma_start(out=raw[c][:], in_=notes_by_word[:, :, starts[c] : starts[c] + CHUNKS[c]])
 
         nc.gpsimd.memset(pool_scales[:].bitcast(I32), 0)
         load_notes(0)
@@ -68,83 +69,89 @@ def tile_attend_tab_looked_runsput_kernel(tc, keys_words, keys_scales, notes, ol
         for t in range(ROW_TILES):
             nc.sync.dma_start(out=prev[t][:], in_=old[t * P : (t + 1) * P, :])
 
-        placed = [keep.tile([P, M], F32, name=f"placed{t}") for t in range(ROW_TILES)]
-        for t in range(ROW_TILES):
-            nc.gpsimd.memset(placed[t][:], 0.0)
+        placed = [keep.tile([P, M], F32, name=f"placed{b}") for b in range(2)]
+        for window in placed:
+            nc.gpsimd.memset(window[:], 0.0)
 
         wide = [keep.tile([P, U], F32, name=f"wide{t}") for t in range(ROW_TILES)]
-        note_words = [keep.tile([P, w], U32, name=f"note_words{c}", align_bytes=64) for c, w in enumerate(CHUNKS)]
-        note_scales = [keep.tile([P, w], U8, name=f"note_scales{c}", align_bytes=64) for c, w in enumerate(CHUNKS)]
-        sums = {}
+        note_words = [keep.tile([P, width], U32, name=f"note_words{c}", align_bytes=64) for c, width in enumerate(CHUNKS)]
+        note_scales = [keep.tile([P, width], U8, name=f"note_scales{c}", align_bytes=64) for c, width in enumerate(CHUNKS)]
 
         def quantise(c):
-            w = CHUNKS[c]
-            grouped = keep.tile([P, w, PACK], BF16, name=f"grouped{c}", align_bytes=64)
-            nc.vector.tensor_copy(
-                out=grouped[:].rearrange("p (c i) t -> p c t i", i=4),
-                in_=raw[c][:].rearrange("p t (c i) -> p c t i", i=4),
-            )
-            nc.vector.quantize_mx(
-                out=note_words[c][:].bitcast(FP8X4),
-                scales=note_scales[c][:],
-                in_=grouped[:].rearrange("p w t -> p (w t)"),
-            )
-
-        SPAN = 256
-        banks = {
-            (g, h): psum.tile([P, BANK], F32, name=f"bank{g}_{h}") for g in range(U // SPAN) for h in range(ROW_TILES // 2)
-        }
-
-        def multiply(c):
-            w = CHUNKS[c]
-            g, inner = divmod(starts[c], SPAN)
-            for t in range(ROW_TILES):
-                first = (t % 2) * SPAN + inner
-                rows = slice(t * P, (t + 1) * P)
-                nc.tensor.matmul_mx(
-                    out=banks[g, t // 2][:, first : first + w],
-                    lhsT=key_words[:, rows].bitcast(FP8X4),
-                    lhsT_scale=key_scales[:, rows],
-                    rhs=note_words[c][:].bitcast(FP8X4),
-                    rhs_scale=note_scales[c][:],
-                    start=True,
-                    stop=True,
+            half = CHUNKS[c] // 2
+            grouped = [keep.tile([P, half, PACK], BF16, name=f"grouped{c}_{h}", align_bytes=64) for h in range(2)]
+            for h in range(2):
+                cast = nc.scalar.copy if (h == 1 and c != 1) else nc.vector.tensor_copy
+                cast(
+                    out=grouped[h][:].rearrange("p (c i) t -> p c t i", i=4),
+                    in_=raw[c][:, :, h * half : (h + 1) * half].rearrange("p t (c i) -> p c t i", i=4),
                 )
+            return grouped
 
-        def evacuate(g, t):
-            source = banks[g, t // 2][:, (t % 2) * SPAN : (t % 2 + 1) * SPAN]
-            target = wide[t][:, g * SPAN : (g + 1) * SPAN]
-            if g == U // SPAN - 1 and t > 0:
-                nc.vector.tensor_copy(out=target, in_=source)
-            else:
-                nc.scalar.copy(out=target, in_=source)
+        def quantise_half(c, h, grouped):
+            half = CHUNKS[c] // 2
+            cols = slice(h * half, (h + 1) * half)
+            nc.vector.quantize_mx(
+                out=note_words[c][:, cols].bitcast(FP8X4),
+                scales=note_scales[c][:, cols],
+                in_=grouped[h][:].rearrange("p w t -> p (w t)"),
+            )
 
-        quantise(0)
+        banks = [[psum.tile([P, BANK], F32, name=f"bank{t}_{h}") for h in range(U // BANK)] for t in range(ROW_TILES)]
+
+        def sums(c, t):
+            h, first = divmod(starts[c], BANK)
+            return banks[t][h][:, first : first + CHUNKS[c]]
+
+        def multiply(c, t):
+            rows = slice(t * P, (t + 1) * P)
+            nc.tensor.matmul_mx(
+                out=sums(c, t),
+                lhsT=key_words[:, rows].bitcast(FP8X4),
+                lhsT_scale=key_scales[:, rows],
+                rhs=note_words[c][:].bitcast(FP8X4),
+                rhs_scale=note_scales[c][:],
+                start=True,
+                stop=True,
+            )
+
+        grouped = quantise(0)
+        quantise_half(0, 0, grouped)
         nc.vector.tensor_copy(key_scales[:], pool_scales[:].indirect(idx[:]))
+        quantise_half(0, 1, grouped)
+        per_tile = P // 16
         for t in range(ROW_TILES):
-            nc.vector.tensor_copy(key_words[:, t * P : (t + 1) * P], pool_words[:].indirect(idx[:, t * 8 : (t + 1) * 8]))
-        for c in range(len(CHUNKS)):
-            if c > 0:
-                quantise(c)
-            multiply(c)
+            nc.vector.tensor_copy(
+                key_words[:, t * P : (t + 1) * P], pool_words[:].indirect(idx[:, t * per_tile : (t + 1) * per_tile])
+            )
+            multiply(0, t)
+        for c in range(1, len(CHUNKS)):
+            grouped = quantise(c)
+            for h in range(2):
+                quantise_half(c, h, grouped)
+            for t in range(ROW_TILES):
+                multiply(c, t)
+            nc.scalar.copy(out=wide[0][:, starts[c] : starts[c] + CHUNKS[c]], in_=sums(c, 0))
+        for t in range(ROW_TILES):
+            nc.scalar.copy(out=wide[t][:, :BANK], in_=banks[t][0][:])
+        for t in range(2, ROW_TILES):
+            nc.vector.tensor_copy(out=wide[t][:, BANK:], in_=banks[t][1][:])
 
-        second = [keep.tile([P, J], F32, name=f"second{t}") for t in range(ROW_TILES)]
-        diff = [keep.tile([P, J], F32, name=f"diff{t}") for t in range(ROW_TILES)]
+        second = {t: keep.tile([P, J], F32, name=f"second{t}")[:] for t in range(2)}
+        diff = [keep.tile([P, J], F32, name=f"diff{t}", tag=f"stage{t}") for t in range(ROW_TILES)]
         best = [keep.tile([P, N], F32, name=f"best{t}") for t in range(ROW_TILES)]
         result = [keep.tile([P, M], F32, name=f"result{t}") for t in range(ROW_TILES)]
 
-        minuend = keep.tile([P, J], F32, name="minuend")
-        last = ROW_TILES - 1
-
-        def look_up(t, lo, hi):
+        def look_up(t, lo, hi, minuend):
             cols = slice(lo, hi)
             entries = slice(lo // 16, hi // 16)
             nc.scalar.activation(second[t][:, cols], wide[t][:].indirect(idx3[:, entries]), COPY)
-            if t == last:
-                nc.scalar.activation(minuend[:, cols], wide[t][:].indirect(idx2[:, entries]), COPY)
-                nc.vector.tensor_tensor(diff[t][:, cols], minuend[:, cols], second[t][:, cols], ALU.subtract)
+            if minuend is None:
+                first = wide[t][:].indirect(idx2[:, entries])
             else:
-                nc.vector.tensor_tensor(diff[t][:, cols], wide[t][:].indirect(idx2[:, entries]), second[t][:, cols], ALU.subtract)
+                nc.scalar.activation(minuend[:, cols], wide[t][:].indirect(idx2[:, entries]), COPY)
+                first = minuend[:, cols]
+            nc.vector.tensor_tensor(diff[t][:, cols], first, second[t][:, cols], ALU.subtract)
 
         def largest(t, lo, hi):
             nc.vector.tensor_reduce(
@@ -155,25 +162,29 @@ def tile_attend_tab_looked_runsput_kernel(tc, keys_words, keys_scales, notes, ol
             )
 
         def place(t):
-            nc.scalar.activation(placed[t][:].indirect(idx4[:]), best[t][:], COPY)
+            nc.scalar.activation(placed[t % 2][:].indirect(idx4[:]), best[t][:], COPY)
 
         def finish(t, lo, hi, queue):
-            nc.vector.tensor_tensor(result[t][:, lo:hi], prev[t][:, lo:hi], placed[t][:, lo:hi], ALU.add)
+            nc.vector.tensor_tensor(result[t][:, lo:hi], prev[t][:, lo:hi], placed[t % 2][:, lo:hi], ALU.add)
             queue.dma_start(out=out[t * P : (t + 1) * P, lo:hi], in_=result[t][:, lo:hi])
 
         for t in range(ROW_TILES):
-            evacuate(U // SPAN - 1, t)
-        for t in range(ROW_TILES):
-            for g in range(U // SPAN - 1):
-                evacuate(g, t)
-            halves = [(0, J // 2), (J // 2, J)] if t in (0, last) else [(0, J)]
-            for lo, hi in halves:
-                look_up(t, lo, hi)
-            if 0 < t < last:
+            minuend = None
+            if t == 1:
+                nc.scalar.copy(out=wide[t][:, BANK:], in_=banks[t][1][:])
+            if t == 2:
+                pair = keep.tile([P, 2 * J], F32, name="pair", tag="stage0")
+                second[2], second[3] = pair[:, :J], pair[:, J:]
+            if t == LAST:
+                minuend = keep.tile([P, J], F32, name="minuend", tag="stage1")
+            parts = [(0, J // 2), (J // 2, J)] if t in (0, LAST) else [(0, J)]
+            for lo, hi in parts:
+                look_up(t, lo, hi, minuend)
+            if 0 < t < LAST:
                 finish(t - 1, 0, M, nc.sync)
-            for lo, hi in halves:
+            for lo, hi in parts:
                 largest(t, lo, hi)
             place(t)
-        finish(last - 1, 0, M, nc.sync)
-        finish(last, 0, M // 2, nc.sync)
-        finish(last, M // 2, M, nc.scalar)
+        finish(LAST - 1, 0, M, nc.sync)
+        finish(LAST, 0, M // 2, nc.sync)
+        finish(LAST, M // 2, M, nc.scalar)

@@ -22,6 +22,7 @@ RUN = J // N
 ROW_TILES = I // P
 LAST = ROW_TILES - 1
 CHUNKS = (512, 256, 256)
+PIECE = 128
 
 
 def tile_attend_tab_looked_runsput_kernel(tc, keys_words, keys_scales, notes, old, offs, offs2, offs3, offs4, out):
@@ -77,63 +78,71 @@ def tile_attend_tab_looked_runsput_kernel(tc, keys_words, keys_scales, notes, ol
         note_words = [keep.tile([P, width], U32, name=f"note_words{c}", align_bytes=64) for c, width in enumerate(CHUNKS)]
         note_scales = [keep.tile([P, width], U8, name=f"note_scales{c}", align_bytes=64) for c, width in enumerate(CHUNKS)]
 
-        def quantise(c):
-            half = CHUNKS[c] // 2
-            grouped = [keep.tile([P, half, PACK], BF16, name=f"grouped{c}_{h}", align_bytes=64) for h in range(2)]
-            for h in range(2):
-                cast = nc.scalar.copy if (h == 1 and c != 1) else nc.vector.tensor_copy
-                cast(
-                    out=grouped[h][:].rearrange("p (c i) t -> p c t i", i=4),
-                    in_=raw[c][:, :, h * half : (h + 1) * half].rearrange("p t (c i) -> p c t i", i=4),
-                )
-            return grouped
+        grouped = {}
 
-        def quantise_half(c, h, grouped):
-            half = CHUNKS[c] // 2
-            cols = slice(h * half, (h + 1) * half)
+        def cast(c, piece, copy):
+            grouped[c, piece] = keep.tile([P, PIECE, PACK], BF16, name=f"grouped{c}_{piece}", align_bytes=64)
+            copy(
+                out=grouped[c, piece][:].rearrange("p (c i) t -> p c t i", i=4),
+                in_=raw[c][:, :, piece * PIECE : (piece + 1) * PIECE].rearrange("p t (c i) -> p c t i", i=4),
+            )
+
+        def quantise(c, piece):
+            cols = slice(piece * PIECE, (piece + 1) * PIECE)
             nc.vector.quantize_mx(
                 out=note_words[c][:, cols].bitcast(FP8X4),
                 scales=note_scales[c][:, cols],
-                in_=grouped[h][:].rearrange("p w t -> p (w t)"),
+                in_=grouped[c, piece][:].rearrange("p w t -> p (w t)"),
             )
 
-        banks = [[psum.tile([P, BANK], F32, name=f"bank{t}_{h}") for h in range(U // BANK)] for t in range(ROW_TILES)]
+        banks = [
+            [psum.tile([P, BANK], F32, name=f"bank{t}_{h}", tag=f"bank{t}_{h}") for h in range(U // BANK)]
+            for t in range(ROW_TILES)
+        ]
 
         def sums(c, t):
             h, first = divmod(starts[c], BANK)
             return banks[t][h][:, first : first + CHUNKS[c]]
 
-        def multiply(c, t):
+        def multiply(target, c, t, cols):
             rows = slice(t * P, (t + 1) * P)
             nc.tensor.matmul_mx(
-                out=sums(c, t),
+                out=target[:, cols],
                 lhsT=key_words[:, rows].bitcast(FP8X4),
                 lhsT_scale=key_scales[:, rows],
-                rhs=note_words[c][:].bitcast(FP8X4),
-                rhs_scale=note_scales[c][:],
+                rhs=note_words[c][:, cols].bitcast(FP8X4),
+                rhs_scale=note_scales[c][:, cols],
                 start=True,
                 stop=True,
             )
 
-        grouped = quantise(0)
-        quantise_half(0, 0, grouped)
+        for piece in range(CHUNKS[0] // PIECE):
+            cast(0, piece, nc.vector.tensor_copy if piece == 0 else nc.scalar.copy)
         nc.vector.tensor_copy(key_scales[:], pool_scales[:].indirect(idx[:]))
-        quantise_half(0, 1, grouped)
+        for piece in range(CHUNKS[0] // PIECE):
+            quantise(0, piece)
         per_tile = P // 16
         for t in range(ROW_TILES):
             nc.vector.tensor_copy(
                 key_words[:, t * P : (t + 1) * P], pool_words[:].indirect(idx[:, t * per_tile : (t + 1) * per_tile])
             )
-            multiply(0, t)
-        for c in range(1, len(CHUNKS)):
-            grouped = quantise(c)
-            for h in range(2):
-                quantise_half(c, h, grouped)
-            for t in range(ROW_TILES):
-                multiply(c, t)
-            nc.scalar.copy(out=wide[0][:, starts[c] : starts[c] + CHUNKS[c]], in_=sums(c, 0))
-        for t in range(ROW_TILES):
+            multiply(sums(0, t), 0, t, slice(0, CHUNKS[0]))
             nc.scalar.copy(out=wide[t][:, :BANK], in_=banks[t][0][:])
+        final = len(CHUNKS) - 1
+        for c in range(1, len(CHUNKS)):
+            pieces = range(CHUNKS[c] // PIECE)
+            for piece in pieces:
+                cast(c, piece, nc.vector.tensor_copy)
+            if c == final:
+                head = psum.tile([P, BANK], F32, name="head", tag="bank0_0")[:, : CHUNKS[c]]
+            else:
+                head = sums(c, 0)
+            for piece in pieces:
+                quantise(c, piece)
+                multiply(head, c, 0, slice(piece * PIECE, (piece + 1) * PIECE))
+            nc.scalar.copy(out=wide[0][:, starts[c] : starts[c] + CHUNKS[c]], in_=head)
+            for t in range(1, ROW_TILES):
+                multiply(sums(c, t), c, t, slice(0, CHUNKS[c]))
         for t in range(2, ROW_TILES):
             nc.vector.tensor_copy(out=wide[t][:, BANK:], in_=banks[t][1][:])
 

from contextlib import ExitStack

import concourse.mybir as mybir

D, T, I, J, U, M, N = 512, 2048, 512, 512, 1024, 512, 64
FLOPS = 2 * D * I * U

F32 = mybir.dt.float32
BF16 = mybir.dt.bfloat16
I32 = mybir.dt.int32
U32 = mybir.dt.uint32
U16 = mybir.dt.uint16
U8 = mybir.dt.uint8
FP8X4 = mybir.dt.float8_e4m3fn_x4
ALU = mybir.AluOpType
COPY = mybir.ActivationFunctionType.Copy

P = 128
PACK = 4
BANK = 512
RUN = J // N
ROW_TILES = I // P
LAST = ROW_TILES - 1
CHUNKS = (512, 256, 256)
PIECE = 128


def tile_attend_tab_looked_runsput_kernel(tc, keys_words, keys_scales, notes, old, offs, offs2, offs3, offs4, out):
    nc = tc.nc
    with ExitStack() as ctx:
        lists = ctx.enter_context(tc.tile_pool(name="lists", bufs=1))
        keep = ctx.enter_context(tc.tile_pool(name="keep", bufs=1))
        psum = ctx.enter_context(tc.psum_pool(name="psum", bufs=1))

        idx = lists.tile([P, I // 16], U16, name="idx")
        idx2 = lists.tile([P, J // 16], U16, name="idx2")
        idx3 = lists.tile([P, J // 16], U16, name="idx3")
        idx4 = lists.tile([P, N // 16], U16, name="idx4")

        pool_words = keep.tile([P, T], U32, name="pool_words", align_bytes=64)
        pool_scales = keep.tile([P, T], U8, name="pool_scales", align_bytes=64)
        key_words = keep.tile([P, I], U32, name="key_words", align_bytes=64)
        key_scales = keep.tile([P, I], U8, name="key_scales", align_bytes=64)

        starts = [sum(CHUNKS[:c]) for c in range(len(CHUNKS))]
        raw = [keep.tile([P, PACK, width], F32, name=f"raw{c}") for c, width in enumerate(CHUNKS)]
        notes_by_word = notes.rearrange("(p j) u -> p j u", j=PACK)

        def load_notes(c):
            nc.sync.dma_start(out=raw[c][:], in_=notes_by_word[:, :, starts[c] : starts[c] + CHUNKS[c]])

        nc.gpsimd.memset(pool_scales[:].bitcast(I32), 0)
        load_notes(0)
        for q in range(4):
            nc.sync.dma_start(
                out=pool_scales[32 * q : 32 * q + 4, :].bitcast(I32),
                in_=keys_scales[0, 4 * q : 4 * q + 4, :].bitcast(I32),
            )
        nc.sync.dma_start(idx[:], offs)
        nc.sync.dma_start(
            out=pool_words[:].bitcast(I32),
            in_=keys_words[0].rearrange("p n t -> p (n t)").bitcast(I32),
        )
        for c in range(1, len(CHUNKS)):
            load_notes(c)
        nc.sync.dma_start(idx3[:], offs3)
        nc.sync.dma_start(idx2[:], offs2)
        nc.sync.dma_start(idx4[:], offs4)
        prev = [keep.tile([P, M], F32, name=f"prev{t}") for t in range(ROW_TILES)]
        for t in range(ROW_TILES):
            nc.sync.dma_start(out=prev[t][:], in_=old[t * P : (t + 1) * P, :])

        placed = [keep.tile([P, M], F32, name=f"placed{b}") for b in range(2)]
        for window in placed:
            nc.gpsimd.memset(window[:], 0.0)

        wide = [keep.tile([P, U], F32, name=f"wide{t}") for t in range(ROW_TILES)]
        note_words = [keep.tile([P, width], U32, name=f"note_words{c}", align_bytes=64) for c, width in enumerate(CHUNKS)]
        note_scales = [keep.tile([P, width], U8, name=f"note_scales{c}", align_bytes=64) for c, width in enumerate(CHUNKS)]

        grouped = {}

        def cast(c, piece, copy):
            grouped[c, piece] = keep.tile([P, PIECE, PACK], BF16, name=f"grouped{c}_{piece}", align_bytes=64)
            copy(
                out=grouped[c, piece][:].rearrange("p (c i) t -> p c t i", i=4),
                in_=raw[c][:, :, piece * PIECE : (piece + 1) * PIECE].rearrange("p t (c i) -> p c t i", i=4),
            )

        def quantise(c, piece):
            cols = slice(piece * PIECE, (piece + 1) * PIECE)
            nc.vector.quantize_mx(
                out=note_words[c][:, cols].bitcast(FP8X4),
                scales=note_scales[c][:, cols],
                in_=grouped[c, piece][:].rearrange("p w t -> p (w t)"),
            )

        banks = [
            [psum.tile([P, BANK], F32, name=f"bank{t}_{h}", tag=f"bank{t}_{h}") for h in range(U // BANK)]
            for t in range(ROW_TILES)
        ]

        def sums(c, t):
            h, first = divmod(starts[c], BANK)
            return banks[t][h][:, first : first + CHUNKS[c]]

        def multiply(target, c, t, cols):
            rows = slice(t * P, (t + 1) * P)
            nc.tensor.matmul_mx(
                out=target[:, cols],
                lhsT=key_words[:, rows].bitcast(FP8X4),
                lhsT_scale=key_scales[:, rows],
                rhs=note_words[c][:, cols].bitcast(FP8X4),
                rhs_scale=note_scales[c][:, cols],
                start=True,
                stop=True,
            )

        for piece in range(CHUNKS[0] // PIECE):
            cast(0, piece, nc.vector.tensor_copy if piece == 0 else nc.scalar.copy)
        nc.vector.tensor_copy(key_scales[:], pool_scales[:].indirect(idx[:]))
        for piece in range(CHUNKS[0] // PIECE):
            quantise(0, piece)
        per_tile = P // 16
        for t in range(ROW_TILES):
            nc.vector.tensor_copy(
                key_words[:, t * P : (t + 1) * P], pool_words[:].indirect(idx[:, t * per_tile : (t + 1) * per_tile])
            )
            multiply(sums(0, t), 0, t, slice(0, CHUNKS[0]))
            nc.scalar.copy(out=wide[t][:, :BANK], in_=banks[t][0][:])
        final = len(CHUNKS) - 1
        for c in range(1, len(CHUNKS)):
            pieces = range(CHUNKS[c] // PIECE)
            for piece in pieces:
                cast(c, piece, nc.vector.tensor_copy)
            if c == final:
                head = psum.tile([P, BANK], F32, name="head", tag="bank0_0")[:, : CHUNKS[c]]
            else:
                head = sums(c, 0)
            for piece in pieces:
                quantise(c, piece)
                multiply(head, c, 0, slice(piece * PIECE, (piece + 1) * PIECE))
            nc.scalar.copy(out=wide[0][:, starts[c] : starts[c] + CHUNKS[c]], in_=head)
            for t in range(1, ROW_TILES):
                multiply(sums(c, t), c, t, slice(0, CHUNKS[c]))
        for t in range(2, ROW_TILES):
            nc.vector.tensor_copy(out=wide[t][:, BANK:], in_=banks[t][1][:])

        second = {t: keep.tile([P, J], F32, name=f"second{t}")[:] for t in range(2)}
        diff = [keep.tile([P, J], F32, name=f"diff{t}", tag=f"stage{t}") for t in range(ROW_TILES)]
        best = [keep.tile([P, N], F32, name=f"best{t}") for t in range(ROW_TILES)]
        result = [keep.tile([P, M], F32, name=f"result{t}") for t in range(ROW_TILES)]

        def look_up(t, lo, hi, minuend):
            cols = slice(lo, hi)
            entries = slice(lo // 16, hi // 16)
            nc.scalar.activation(second[t][:, cols], wide[t][:].indirect(idx3[:, entries]), COPY)
            if minuend is None:
                first = wide[t][:].indirect(idx2[:, entries])
            else:
                nc.scalar.activation(minuend[:, cols], wide[t][:].indirect(idx2[:, entries]), COPY)
                first = minuend[:, cols]
            nc.vector.tensor_tensor(diff[t][:, cols], first, second[t][:, cols], ALU.subtract)

        def largest(t, lo, hi):
            nc.vector.tensor_reduce(
                best[t][:, lo // RUN : hi // RUN],
                diff[t][:, lo:hi].rearrange("p (n r) -> p n r", r=RUN),
                axis=mybir.AxisListType.X,
                op=ALU.max,
            )

        def place(t):
            nc.scalar.activation(placed[t % 2][:].indirect(idx4[:]), best[t][:], COPY)

        def finish(t, lo, hi, queue):
            nc.vector.tensor_tensor(result[t][:, lo:hi], prev[t][:, lo:hi], placed[t % 2][:, lo:hi], ALU.add)
            queue.dma_start(out=out[t * P : (t + 1) * P, lo:hi], in_=result[t][:, lo:hi])

        for t in range(ROW_TILES):
            minuend = None
            if t == 1:
                nc.scalar.copy(out=wide[t][:, BANK:], in_=banks[t][1][:])
            if t == 2:
                pair = keep.tile([P, 2 * J], F32, name="pair", tag="stage0")
                second[2], second[3] = pair[:, :J], pair[:, J:]
            if t == LAST:
                minuend = keep.tile([P, J], F32, name="minuend", tag="stage1")
            parts = [(0, J // 2), (J // 2, J)] if t in (0, LAST) else [(0, J)]
            for lo, hi in parts:
                look_up(t, lo, hi, minuend)
            if 0 < t < LAST:
                finish(t - 1, 0, M, nc.sync)
            for lo, hi in parts:
                largest(t, lo, hi)
            place(t)
        finish(LAST - 1, 0, M, nc.sync)
        finish(LAST, 0, M // 2, nc.sync)
        finish(LAST, M // 2, M, nc.scalar)
